import numpy as np
import ml_dtypes


def mxq(x, axis, fmt="e4m3"):
    dtype, down = {"e4m3": (ml_dtypes.float8_e4m3fn, 7), "e5m2": (ml_dtypes.float8_e5m2, 14)}[fmt]
    v = np.moveaxis(np.asarray(x, np.float32).astype(ml_dtypes.bfloat16).astype(np.float64), axis, -1)
    blocks = v.reshape(v.shape[:-1] + (-1, 32))
    amax = np.abs(blocks).max(-1, keepdims=True)
    byte = np.maximum(np.where(amax > 0, np.frexp(amax)[1] - 1 + 127, 0) - down, 1)
    scale = np.exp2(byte - 127.0)
    codes = (blocks / scale).astype(np.float32).astype(dtype).astype(np.float64)
    return np.moveaxis((codes * scale).reshape(v.shape), -1, axis)


WIDE = False


def mx_kscale(k):
    if not WIDE:
        return np.ones(k)
    levels = np.array([10, -10, 5, -5, 0])
    if k % 512:
        return np.exp2(np.random.permutation(np.resize(levels, k // 32))).repeat(32)
    a = np.empty((k // 512, 16))
    for p in range(k // 512):
        a[p, :8] = np.random.permutation(np.resize(levels, 8))
        for g in range(8):
            far = levels[np.abs(levels - a[p, g]) >= 10]
            a[p, g + 8] = far[np.random.randint(len(far))]
    return np.exp2(a.ravel()).repeat(32)


def f64(x):
    return np.asarray(x).astype(np.float64)


def striped(idx):
    return np.tile(idx.reshape(-1, 16).T, (8, 1)).astype(np.uint16)


def unstriped(offs):
    return offs[:16].T.reshape(-1).astype(np.int64)


def striped8(idx):
    return np.concatenate([x.reshape(-1, 16).T for x in idx]).astype(np.uint16)


def runs(offs, k):
    lists = np.stack([offs[16 * r : 16 * r + 16].T.reshape(-1) for r in range(8)]).astype(np.int64)
    return lists[np.arange(k) % 512 // 64]


def pack_weight(w):
    k, n = w.shape
    w = f64(np.asarray(w, np.float32).astype(ml_dtypes.bfloat16)).reshape(k // 32, 32, n)
    amax = np.abs(w).max(1)
    byte = np.clip(np.where(amax > 0, np.frexp(amax)[1] - 1 + 127 - 7, 1), 1, 254)
    scaled = (w * np.exp2(127.0 - byte)[:, None, :]).reshape(k, n).astype(np.float32)
    words = np.ascontiguousarray(scaled.reshape(k // 512, 128, 4, n).transpose(0, 1, 3, 2)).astype(ml_dtypes.float8_e4m3fn).view(np.uint8)
    return words, np.ascontiguousarray(byte.astype(np.uint8).reshape(k // 512, 16, n))


def unpack_weight(words, scales):
    g, p, n, _ = words.shape
    vals = np.ascontiguousarray(words).view(ml_dtypes.float8_e4m3fn).astype(np.float64) * np.repeat(np.exp2(scales.astype(np.float64) - 127.0), 8, axis=1)[..., None]
    return vals.transpose(0, 1, 3, 2).reshape(g * 512, n)


def relu(v):
    return np.maximum(v, 0.0)


K, T, S, N, H, W, U = 512, 2048, 512, 512, 512, 256, 1024


def setup_inputs():
    n = np.random.standard_normal
    s = mx_kscale(K)[:, None]
    u = mx_kscale(S)
    packed_xT = pack_weight(n((K, T)) * s)
    perm = np.stack([np.random.permutation(H) for _ in range(8)])
    return {
        "x_words": packed_xT[0],
        "x_scales": packed_xT[1],
        "wa": (n((K, H)) / np.sqrt(K) / s).astype(np.float32),
        "wb": (n((K, N)) / np.sqrt(K) / s).astype(np.float32),
        "gt": (np.random.uniform(0.5, 1.5, (S, 1)) * u[:, None]).astype(np.float32),
        "gi": (np.random.uniform(0.5, 1.5, (S, 1)) / u[:, None]).astype(np.float32),
        "offs": striped(np.random.permutation(T)[:S]),
        "two": striped(np.random.permutation(T)[:S]),
        "n1": striped8(perm[:, :W]),
        "n2": striped8(perm[:, W:]),
        "n3": striped8(np.stack([np.random.permutation(U)[:N] for _ in range(8)])),
        "n4": striped8(np.stack([np.random.permutation(N) for _ in range(8)])),
    }


def reference(x_words, x_scales, wa, wb, gt, gi, offs, two, n1, n2, n3, n4):
    xq = unpack_weight(x_words, x_scales)[:, unstriped(offs)]
    a = xq.T @ mxq(f64(wa), 0, "e4m3")
    pa = a[np.arange(S)[:, None], runs(n1, S)]
    pb = a[np.arange(S)[:, None], runs(n2, S)]
    rb = np.minimum(pa, pb)
    ra = np.maximum(pa, pb)
    ds = np.zeros((S, H))
    ds[np.arange(S)[:, None], runs(n1, S)] = ra
    dt = ds.copy()
    dt[np.arange(S)[:, None], runs(n2, S)] = rb
    z = f64(gt) * dt
    x_two = unpack_weight(x_words, x_scales)[:, unstriped(two)]
    b = x_two.T @ mxq(f64(wb), 0, "e4m3")
    z2 = f64(gi) * b
    cv = 0.0625 * ((mxq(z, 0, "e4m3").T @ mxq(z2, 0, "e4m3")))
    nw = cv - (relu(cv[np.arange(H)[:, None], runs(n4, H)]))
    out = np.zeros((H, U))
    out[np.arange(H)[:, None], runs(n3, H)] = nw
    return out

@@ -1,0 +1,245 @@
+from contextlib import ExitStack
+
+import concourse.mybir as mybir
+from concourse.masks import make_identity
+
+F32 = mybir.dt.float32
+BF16 = mybir.dt.bfloat16
+I32 = mybir.dt.int32
+U32 = mybir.dt.uint32
+U16 = mybir.dt.uint16
+U8 = mybir.dt.uint8
+FP8X4 = mybir.dt.float8_e4m3fn_x4
+ALU = mybir.AluOpType
+ACT = mybir.ActivationFunctionType
+
+P = 128
+PACK = 4
+T, S, H, N, W, U = 2048, 512, 512, 512, 256, 1024
+CV_SCALE = 0.0625
+
+FLOPS = 2 * 3 * 512 * 512 * 512
+
+
+def tile_picked_momorderpagez_none_p_kernel(
+    tc, x_words, x_scales, wa, wb, gt, gi, offs, two, n1, n2, n3, n4, out
+):
+    nc = tc.nc
+    with ExitStack() as ctx:
+        lists = ctx.enter_context(tc.tile_pool(name="lists", bufs=1))
+        keep = ctx.enter_context(tc.tile_pool(name="keep", bufs=1))
+        psum = ctx.enter_context(tc.psum_pool(name="psum", bufs=1))
+
+        def load_list(name, src):
+            tile = lists.tile(list(src.shape), U16, name=name)
+            nc.sync.dma_start(tile[:], src)
+            return tile
+
+        offs_sb = load_list("offs_sb", offs)
+        two_sb = load_list("two_sb", two)
+
+        scale_table = keep.tile([P, T], U8, name="scale_table", align_bytes=64)
+        nc.vector.memset(scale_table[:].bitcast(I32), 0)
+        for q in range(4):
+            nc.scalar.dma_start(
+                scale_table[32 * q : 32 * q + 4, :].bitcast(I32),
+                x_scales[0][4 * q : 4 * q + 4, :].bitcast(I32),
+            )
+
+        def load_weight_half(w, half):
+            raw = keep.tile([P, PACK, H // 2], F32, name="w_raw", tag=f"w_raw{half}", align_bytes=64)
+            cols = slice(half * (H // 2), (half + 1) * (H // 2))
+            nc.sync.dma_start(raw[:], w.rearrange("(p j) c -> p j c", j=PACK)[:, :, cols])
+            return raw
+
+        def interleave(grouped, raw):
+            nc.scalar.copy(
+                grouped.rearrange("p (c i) j -> p c j i", i=4), raw.rearrange("p j (c i) -> p c j i", i=4)
+            )
+
+        def interleave_weight_half(raw, name):
+            grouped = keep.tile([P, H // 2, PACK], BF16, name=name, tag=name, align_bytes=64)
+            interleave(grouped[:], raw[:])
+            return grouped
+
+        def quantize(codes, scales, grouped):
+            nc.vector.quantize_mx(
+                out=codes.bitcast(FP8X4), scales=scales, in_=grouped.rearrange("p c j -> p (c j)")
+            )
+
+        wa_raw = [load_weight_half(wa, h) for h in range(2)]
+
+        word_table = keep.tile([P, T], U32, name="word_table", align_bytes=64)
+        nc.sync.dma_start(word_table[:].bitcast(I32), x_words[0].rearrange("p n t -> p (n t)").bitcast(I32))
+
+        n1_sb = load_list("n1_sb", n1)
+        n2_sb = load_list("n2_sb", n2)
+
+        ident = keep.tile([P, P], F32, name="ident")
+        make_identity(nc, ident[:])
+        g_rows = keep.tile([P, P], F32, name="g_rows")
+        nc.gpsimd.memset(g_rows[:], 0.0)
+        for i, g in enumerate((gt, gi)):
+            nc.sync.dma_start(
+                g_rows[PACK * i : PACK * (i + 1), :].rearrange("t (b r) -> t b r", r=8),
+                g.rearrange("(b t r) o -> t b (r o)", t=PACK, r=8),
+            )
+        n4_sb = load_list("n4_sb", n4)
+        n3_sb = load_list("n3_sb", n3)
+
+        def blank_page(u, tag):
+            page = keep.tile([P, U], F32, name=f"page{u}", tag=tag, align_bytes=64)
+            nc.vector.memset(page[:].bitcast(I32), 0)
+            return page
+
+        pages = [blank_page(u, f"page{u}") for u in range(2)]
+
+        wa_grouped = [interleave_weight_half(wa_raw[h], f"wa_grouped{h}") for h in range(2)]
+
+        picked_scales = keep.tile([P, 2 * S], U8, name="picked_scales", align_bytes=64)
+        nc.vector.tensor_copy(picked_scales[:, 0:S], scale_table[:].indirect(offs_sb[:]))
+        nc.vector.tensor_copy(picked_scales[:, S : 2 * S], scale_table[:].indirect(two_sb[:]))
+
+        wa_codes = keep.tile([P, H], U32, name="wa_codes", align_bytes=64)
+        wa_scales = keep.tile([P, H], U8, name="wa_scales", align_bytes=64)
+        for h in range(2):
+            cols = slice(h * (H // 2), (h + 1) * (H // 2))
+            quantize(wa_codes[:, cols], wa_scales[:, cols], wa_grouped[h][:])
+
+        dealt_scales = keep.tile([P, 2 * S], U8, name="dealt_scales", align_bytes=64)
+        nc.vector.tensor_copy(
+            dealt_scales[:].bitcast(I32).rearrange("p (l t b w) -> p l t b w", l=2, t=PACK, w=2),
+            picked_scales[:].bitcast(I32).rearrange("p (l b t w) -> p l t b w", l=2, t=PACK, w=2),
+        )
+
+        def pick_words(name, list_sb, tag):
+            picked = keep.tile([P, S], U32, name=name, tag=tag, align_bytes=64)
+            nc.vector.tensor_copy(
+                picked[:].rearrange("p (t b r) -> p b t r", t=PACK, r=8),
+                word_table[:].indirect(list_sb[:]),
+            )
+            return picked
+
+        xa_words = pick_words("xa_words", offs_sb, "xa_words")
+        xb_words = pick_words("xb_words", two_sb, "wa_grouped1")
+
+        def mx(acc, l_codes, l_scales, r_codes, r_scales):
+            nc.tensor.matmul_mx(
+                out=acc, lhsT=l_codes.bitcast(FP8X4), lhsT_scale=l_scales,
+                rhs=r_codes.bitcast(FP8X4), rhs_scale=r_scales, start=True, stop=True,
+            )
+
+        a_sb = []
+        for t in range(PACK):
+            cols = slice(t * P, (t + 1) * P)
+            acc = psum.tile([P, H], F32, name="acc", tag="acc", bufs=4)
+            mx(acc[:], xa_words[:, cols], dealt_scales[:, cols], wa_codes[:], wa_scales[:])
+            a_t = keep.tile([P, H], F32, name=f"a{t}")
+            nc.scalar.copy(a_t[:], acc[:])
+            a_sb.append(a_t)
+
+        wb_raw = [load_weight_half(wb, h) for h in range(2)]
+        wb_grouped = keep.tile([P, N, PACK], BF16, name="wb_grouped", tag="wb_then_dt1", align_bytes=64)
+        for h in range(2):
+            interleave(wb_grouped[:, h * (N // 2) : (h + 1) * (N // 2), :], wb_raw[h][:])
+        g_psum = psum.tile([P, P], F32, name="g_psum")
+        nc.tensor.transpose(g_psum[:], g_rows[:], ident[:])
+        g_cols = keep.tile([P, 2 * PACK], F32, name="g_cols", tag="w_raw1", align_bytes=64)
+        nc.scalar.copy(g_cols[:], g_psum[:, 0 : 2 * PACK])
+        wb_codes = keep.tile([P, N], U32, name="wb_codes", align_bytes=64)
+        wb_scales = keep.tile([P, N], U8, name="wb_scales", align_bytes=64)
+        z2_grouped = keep.tile([P, N, PACK], BF16, name="z2_grouped", align_bytes=64)
+        z2_codes = keep.tile([P, N], U32, name="z2_codes", align_bytes=64)
+        z2_scales = keep.tile([P, N], U8, name="z2_scales", align_bytes=64)
+
+        def second_projection():
+            quantize(wb_codes[:], wb_scales[:], wb_grouped[:])
+            for t in range(PACK):
+                acc_b = psum.tile([P, N], F32, name="acc_b", tag="acc_b", bufs=3)
+                mx(acc_b[:], xb_words[:, t * P : (t + 1) * P], dealt_scales[:, S + t * P : S + (t + 1) * P],
+                   wb_codes[:], wb_scales[:])
+                nc.scalar.activation(z2_grouped[:, :, t], acc_b[:], ACT.Copy, scale=g_cols[:, PACK + t : PACK + t + 1])
+
+        pa = keep.tile([P, W], F32, name="pa")
+        pb = keep.tile([P, W], F32, name="pb")
+        ra = keep.tile([P, W], F32, name="ra")
+        rb = keep.tile([P, W], F32, name="rb")
+        dt = []
+        z_grouped = [keep.tile([P, P, PACK], BF16, name=f"z_grouped{u}", tag=f"z_grouped{u}", align_bytes=64) for u in range(PACK)]
+
+        def fetch_pairs(t):
+            nc.vector.tensor_copy(pa[:], a_sb[t][:].indirect(n1_sb[:]))
+            nc.vector.tensor_copy(pb[:], a_sb[t][:].indirect(n2_sb[:]))
+
+        def order_pairs(t):
+            nc.vector.tensor_tensor(ra[:], pa[:], pb[:], ALU.max)
+            nc.vector.tensor_tensor(rb[:], pa[:], pb[:], ALU.min)
+
+        def round_z(t):
+            by_tile = dt[t][:].rearrange("p (m u) -> p u m", u=PACK)
+            for u in range(PACK):
+                nc.scalar.activation(z_grouped[u][:, :, t], by_tile[:, u, :], ACT.Copy, scale=g_cols[:, t : t + 1])
+
+        fetch_pairs(0)
+        order_pairs(0)
+        for t in range(PACK):
+            dt.append(keep.tile([P, H], F32, name=f"dt{t}", tag="wb_then_dt1" if t == 1 else f"dt{t}", align_bytes=64))
+            nc.vector.tensor_copy(dt[t][:].indirect(n1_sb[:]), ra[:])
+            if t + 1 < PACK:
+                fetch_pairs(t + 1)
+            nc.vector.tensor_copy(dt[t][:].indirect(n2_sb[:]), rb[:])
+            if t + 1 < PACK:
+                order_pairs(t + 1)
+            if t == 0:
+                second_projection()
+            round_z(t)
+
+        quantize(z2_codes[:], z2_scales[:], z2_grouped[:])
+
+        z_codes = [keep.tile([P, P], U32, name=f"z_codes{u}", align_bytes=64) for u in range(PACK)]
+        z_scales = [keep.tile([P, P], U8, name=f"z_scales{u}", align_bytes=64) for u in range(PACK)]
+        cv = [keep.tile([P, N], F32, name=f"cv{u}") for u in range(PACK)]
+        neg_relu = [keep.tile([P, N], F32, name=f"neg_relu{u}") for u in range(PACK)]
+        fetched = [keep.tile([P, N], F32, name=f"fetched{u}") for u in range(PACK)]
+        for u in range(PACK):
+            quantize(z_codes[u][:], z_scales[u][:], z_grouped[u][:])
+            if u < 2:
+                pages.append(blank_page(2 + u, f"z_grouped{u}"))
+            acc = psum.tile([P, N], F32, name="acc", tag="acc", bufs=4)
+            mx(acc[:], z_codes[u][:], z_scales[u][:], z2_codes[:], z2_scales[:])
+            if u == 0:
+                nc.vector.tensor_scalar(neg_relu[u][:], acc[:], -CV_SCALE, 0.0, ALU.mult, ALU.min)
+                nc.scalar.activation(cv[u][:], acc[:], ACT.Copy, scale=CV_SCALE)
+            else:
+                relu = keep.tile([P, N], F32, name="relu", tag="relu", bufs=2)
+                nc.scalar.activation(relu[:], acc[:], ACT.Relu, scale=CV_SCALE)
+                nc.scalar.activation(neg_relu[u][:], relu[:], ACT.Copy, scale=-1.0)
+                nc.scalar.activation(cv[u][:], acc[:], ACT.Copy, scale=CV_SCALE)
+
+        half = N // 2
+        list_cols = half // 16
+
+        def fetch(u, h):
+            nc.vector.tensor_copy(
+                fetched[u][:, h * half : (h + 1) * half],
+                neg_relu[u][:].indirect(n4_sb[:, h * list_cols : (h + 1) * list_cols]),
+            )
+
+        def put(u, h):
+            cols = slice(h * half, (h + 1) * half)
+            nc.vector.tensor_tensor(
+                pages[u][:].indirect(n3_sb[:, h * list_cols : (h + 1) * list_cols]),
+                fetched[u][:, cols], cv[u][:, cols], ALU.add,
+            )
+
+        out_rows = out.rearrange("(m u) w -> u m w", u=PACK)
+        fetch(0, 0)
+        fetch(0, 1)
+        for u in range(PACK):
+            put(u, 0)
+            if u + 1 < PACK:
+                fetch(u + 1, 0)
+            put(u, 1)
+            if u + 1 < PACK:
+                fetch(u + 1, 1)
+            nc.sync.dma_start(out_rows[u], pages[u][:])

@@ -39,13 +39,8 @@ def tile_picked_momorderpagez_none_p_kernel(
         two_sb = load_list("two_sb", two)
 
         scale_table = keep.tile([P, T], U8, name="scale_table", align_bytes=64)
-        nc.vector.memset(scale_table[:].bitcast(I32), 0)
-        for q in range(4):
-            nc.scalar.dma_start(
-                scale_table[32 * q : 32 * q + 4, :].bitcast(I32),
-                x_scales[0][4 * q : 4 * q + 4, :].bitcast(I32),
-            )
-
+        nc.vector.memset(scale_table[:, 0 : T // 2].bitcast(I32), 0)
+        nc.gpsimd.memset(scale_table[:, T // 2 : T].bitcast(I32), 0)
         def load_weight_half(w, half):
             raw = keep.tile([P, PACK, H // 2], F32, name="w_raw", tag=f"w_raw{half}", align_bytes=64)
             cols = slice(half * (H // 2), (half + 1) * (H // 2))
@@ -67,9 +62,15 @@ def tile_picked_momorderpagez_none_p_kernel(
                 out=codes.bitcast(FP8X4), scales=scales, in_=grouped.rearrange("p c j -> p (c j)")
             )
 
-        wa_raw = [load_weight_half(wa, h) for h in range(2)]
+        wa_raw = [load_weight_half(wa, 0)]
+        for q in range(4):
+            nc.sync.dma_start(
+                scale_table[32 * q : 32 * q + 4, :].bitcast(I32),
+                x_scales[0][4 * q : 4 * q + 4, :].bitcast(I32),
+            )
+        wa_raw.append(load_weight_half(wa, 1))
 
-        word_table = keep.tile([P, T], U32, name="word_table", align_bytes=64)
+        word_table = keep.tile([P, T], U32, name="word_table", tag="word_table", align_bytes=64)
         nc.sync.dma_start(word_table[:].bitcast(I32), x_words[0].rearrange("p n t -> p (n t)").bitcast(I32))
 
         n1_sb = load_list("n1_sb", n1)
@@ -87,30 +88,39 @@ def tile_picked_momorderpagez_none_p_kernel(
         n4_sb = load_list("n4_sb", n4)
         n3_sb = load_list("n3_sb", n3)
 
-        def blank_page(u, tag):
-            page = keep.tile([P, U], F32, name=f"page{u}", tag=tag, align_bytes=64)
-            nc.vector.memset(page[:].bitcast(I32), 0)
-            return page
+        pages = [keep.tile([P, U], F32, name="page0")]
+        nc.vector.memset(pages[0][:].bitcast(I32), 0)
 
-        pages = [blank_page(u, f"page{u}") for u in range(2)]
+        def blank_page(tag):
+            page = keep.tile([P, U], F32, name="page", tag=tag, align_bytes=64)
+            nc.sync.dma_start(page[:], pages[0][:])
+            pages.append(page)
 
         wa_grouped = [interleave_weight_half(wa_raw[h], f"wa_grouped{h}") for h in range(2)]
 
-        picked_scales = keep.tile([P, 2 * S], U8, name="picked_scales", align_bytes=64)
-        nc.vector.tensor_copy(picked_scales[:, 0:S], scale_table[:].indirect(offs_sb[:]))
-        nc.vector.tensor_copy(picked_scales[:, S : 2 * S], scale_table[:].indirect(two_sb[:]))
+        def pick_scales(name, list_sb, tag):
+            picked = keep.tile([P, S], U8, name="picked", tag=tag, align_bytes=64)
+            nc.vector.tensor_copy(picked[:], scale_table[:].indirect(list_sb[:]))
+            dealt = keep.tile([P, S], U8, name=name, align_bytes=64)
+            return picked, dealt
 
-        wa_codes = keep.tile([P, H], U32, name="wa_codes", align_bytes=64)
+        def deal_scales(picked, dealt):
+            nc.vector.tensor_copy(
+                dealt[:].bitcast(I32).rearrange("p (t b w) -> p t b w", t=PACK, w=2),
+                picked[:].bitcast(I32).rearrange("p (b t w) -> p t b w", t=PACK, w=2),
+            )
+
+        xa_picked, xa_scales = pick_scales("xa_scales", offs_sb, "xa_picked")
+        xb_picked, xb_scales = pick_scales("xb_scales", two_sb, "xb_picked")
+
+        wa_codes = keep.tile([P, H], U32, name="wa_codes", tag="wa_codes", align_bytes=64)
         wa_scales = keep.tile([P, H], U8, name="wa_scales", align_bytes=64)
         for h in range(2):
             cols = slice(h * (H // 2), (h + 1) * (H // 2))
             quantize(wa_codes[:, cols], wa_scales[:, cols], wa_grouped[h][:])
 
-        dealt_scales = keep.tile([P, 2 * S], U8, name="dealt_scales", align_bytes=64)
-        nc.vector.tensor_copy(
-            dealt_scales[:].bitcast(I32).rearrange("p (l t b w) -> p l t b w", l=2, t=PACK, w=2),
-            picked_scales[:].bitcast(I32).rearrange("p (l b t w) -> p l t b w", l=2, t=PACK, w=2),
-        )
+        deal_scales(xa_picked, xa_scales)
+        deal_scales(xb_picked, xb_scales)
 
         def pick_words(name, list_sb, tag):
             picked = keep.tile([P, S], U32, name=name, tag=tag, align_bytes=64)
@@ -120,8 +130,8 @@ def tile_picked_momorderpagez_none_p_kernel(
             )
             return picked
 
-        xa_words = pick_words("xa_words", offs_sb, "xa_words")
-        xb_words = pick_words("xb_words", two_sb, "wa_grouped1")
+        xa_words = pick_words("xa_words", offs_sb, "xa_wb_dt1")
+        xb_words = pick_words("xb_words", two_sb, "xb_words")
 
         def mx(acc, l_codes, l_scales, r_codes, r_scales):
             nc.tensor.matmul_mx(
@@ -132,14 +142,15 @@ def tile_picked_momorderpagez_none_p_kernel(
         a_sb = []
         for t in range(PACK):
             cols = slice(t * P, (t + 1) * P)
-            acc = psum.tile([P, H], F32, name="acc", tag="acc", bufs=4)
-            mx(acc[:], xa_words[:, cols], dealt_scales[:, cols], wa_codes[:], wa_scales[:])
-            a_t = keep.tile([P, H], F32, name=f"a{t}")
-            nc.scalar.copy(a_t[:], acc[:])
+            a_t = keep.tile([P, H], F32, name=f"a{t}", tag=f"a{t}", align_bytes=64)
+            for part in ((slice(0, H // 2), slice(H // 2, H)) if t == 0 else (slice(0, H),)):
+                acc = psum.tile([P, part.stop - part.start], F32, name="acc", tag="acc", bufs=4)
+                mx(acc[:], xa_words[:, cols], xa_scales[:, cols], wa_codes[:, part], wa_scales[:, part])
+                nc.scalar.copy(a_t[:, part], acc[:])
             a_sb.append(a_t)
 
         wb_raw = [load_weight_half(wb, h) for h in range(2)]
-        wb_grouped = keep.tile([P, N, PACK], BF16, name="wb_grouped", tag="wb_then_dt1", align_bytes=64)
+        wb_grouped = keep.tile([P, N, PACK], BF16, name="wb_grouped", tag="xa_wb_dt1", align_bytes=64)
         for h in range(2):
             interleave(wb_grouped[:, h * (N // 2) : (h + 1) * (N // 2), :], wb_raw[h][:])
         g_psum = psum.tile([P, P], F32, name="g_psum")
@@ -156,7 +167,7 @@ def tile_picked_momorderpagez_none_p_kernel(
             quantize(wb_codes[:], wb_scales[:], wb_grouped[:])
             for t in range(PACK):
                 acc_b = psum.tile([P, N], F32, name="acc_b", tag="acc_b", bufs=3)
-                mx(acc_b[:], xb_words[:, t * P : (t + 1) * P], dealt_scales[:, S + t * P : S + (t + 1) * P],
+                mx(acc_b[:], xb_words[:, t * P : (t + 1) * P], xb_scales[:, t * P : (t + 1) * P],
                    wb_codes[:], wb_scales[:])
                 nc.scalar.activation(z2_grouped[:, :, t], acc_b[:], ACT.Copy, scale=g_cols[:, PACK + t : PACK + t + 1])
 
@@ -183,7 +194,7 @@ def tile_picked_momorderpagez_none_p_kernel(
         fetch_pairs(0)
         order_pairs(0)
         for t in range(PACK):
-            dt.append(keep.tile([P, H], F32, name=f"dt{t}", tag="wb_then_dt1" if t == 1 else f"dt{t}", align_bytes=64))
+            dt.append(keep.tile([P, H], F32, name=f"dt{t}", tag="xa_wb_dt1" if t == 1 else f"dt{t}", align_bytes=64))
             nc.vector.tensor_copy(dt[t][:].indirect(n1_sb[:]), ra[:])
             if t + 1 < PACK:
                 fetch_pairs(t + 1)
@@ -192,54 +203,59 @@ def tile_picked_momorderpagez_none_p_kernel(
                 order_pairs(t + 1)
             if t == 0:
                 second_projection()
+                for tag in ("w_raw0", "wa_codes", "a0"):
+                    blank_page(tag)
             round_z(t)
 
         quantize(z2_codes[:], z2_scales[:], z2_grouped[:])
 
         z_codes = [keep.tile([P, P], U32, name=f"z_codes{u}", align_bytes=64) for u in range(PACK)]
         z_scales = [keep.tile([P, P], U8, name=f"z_scales{u}", align_bytes=64) for u in range(PACK)]
-        cv = [keep.tile([P, N], F32, name=f"cv{u}") for u in range(PACK)]
         neg_relu = [keep.tile([P, N], F32, name=f"neg_relu{u}") for u in range(PACK)]
         fetched = [keep.tile([P, N], F32, name=f"fetched{u}") for u in range(PACK)]
+        half = N // 2
+        halves = [slice(h * half, (h + 1) * half) for h in range(2)]
+        sums = []
+        cv = []
+
+        def copy_cv(u):
+            cv_u = keep.tile([P, N], F32, name="cv", tag=f"relu{u + 1}")
+            for cols, acc in sums[u]:
+                nc.scalar.activation(cv_u[:, cols], acc[:], ACT.Copy, scale=CV_SCALE)
+            cv.append(cv_u)
+
         for u in range(PACK):
             quantize(z_codes[u][:], z_scales[u][:], z_grouped[u][:])
-            if u < 2:
-                pages.append(blank_page(2 + u, f"z_grouped{u}"))
-            acc = psum.tile([P, N], F32, name="acc", tag="acc", bufs=4)
-            mx(acc[:], z_codes[u][:], z_scales[u][:], z2_codes[:], z2_scales[:])
             if u == 0:
-                nc.vector.tensor_scalar(neg_relu[u][:], acc[:], -CV_SCALE, 0.0, ALU.mult, ALU.min)
-                nc.scalar.activation(cv[u][:], acc[:], ACT.Copy, scale=CV_SCALE)
+                sums.append([])
+                for cols in halves:
+                    acc = psum.tile([P, half], F32, name="acc_b", tag="acc_b", bufs=3)
+                    mx(acc[:], z_codes[u][:], z_scales[u][:], z2_codes[:, cols], z2_scales[:, cols])
+                    nc.vector.tensor_scalar(neg_relu[u][:, cols], acc[:], -CV_SCALE, 0.0, ALU.mult, ALU.min)
+                    sums[u].append((cols, acc))
             else:
-                relu = keep.tile([P, N], F32, name="relu", tag="relu", bufs=2)
+                acc = psum.tile([P, N], F32, name="acc", tag="acc", bufs=4)
+                mx(acc[:], z_codes[u][:], z_scales[u][:], z2_codes[:], z2_scales[:])
+                sums.append([(slice(0, N), acc)])
+                relu = keep.tile([P, N], F32, name="relu", tag=f"relu{u}")
                 nc.scalar.activation(relu[:], acc[:], ACT.Relu, scale=CV_SCALE)
                 nc.scalar.activation(neg_relu[u][:], relu[:], ACT.Copy, scale=-1.0)
-                nc.scalar.activation(cv[u][:], acc[:], ACT.Copy, scale=CV_SCALE)
+                copy_cv(u - 1)
+        copy_cv(PACK - 1)
 
-        half = N // 2
         list_cols = half // 16
 
-        def fetch(u, h):
-            nc.vector.tensor_copy(
-                fetched[u][:, h * half : (h + 1) * half],
-                neg_relu[u][:].indirect(n4_sb[:, h * list_cols : (h + 1) * list_cols]),
-            )
-
-        def put(u, h):
-            cols = slice(h * half, (h + 1) * half)
-            nc.vector.tensor_tensor(
-                pages[u][:].indirect(n3_sb[:, h * list_cols : (h + 1) * list_cols]),
-                fetched[u][:, cols], cv[u][:, cols], ALU.add,
-            )
+        def fetch(u):
+            for h in range(2):
+                nc.vector.tensor_copy(
+                    fetched[u][:, halves[h]],
+                    neg_relu[u][:].indirect(n4_sb[:, h * list_cols : (h + 1) * list_cols]),
+                )
 
         out_rows = out.rearrange("(m u) w -> u m w", u=PACK)
-        fetch(0, 0)
-        fetch(0, 1)
+        fetch(0)
         for u in range(PACK):
-            put(u, 0)
             if u + 1 < PACK:
-                fetch(u + 1, 0)
-            put(u, 1)
-            if u + 1 < PACK:
-                fetch(u + 1, 1)
+                fetch(u + 1)
+            nc.vector.tensor_tensor(pages[u][:].indirect(n3_sb[:]), fetched[u][:], cv[u][:], ALU.add)
             nc.sync.dma_start(out_rows[u], pages[u][:])

@@ -15,10 +15,20 @@ ACT = mybir.ActivationFunctionType
 
 P = 128
 PACK = 4
-T, S, H, N, W, U = 2048, 512, 512, 512, 256, 1024
+RUN = 8
+QUADRANT = 32
+LIST_ROWS = 16
+T = 2048
+S = 512
+C = 512
+PAIRS = 256
+PAGE = 1024
 CV_SCALE = 0.0625
+HALVES = (slice(0, C // 2), slice(C // 2, C))
+WIDE_BANKS = 4
+SIDE_BANKS = 3
 
-FLOPS = 2 * 3 * 512 * 512 * 512
+FLOPS = 3 * 2 * 512 * 512 * 512
 
 
 def tile_picked_momorderpagez_none_p_kernel(
@@ -31,20 +41,13 @@ def tile_picked_momorderpagez_none_p_kernel(
         psum = ctx.enter_context(tc.psum_pool(name="psum", bufs=1))
 
         def load_list(name, src):
-            tile = lists.tile(list(src.shape), U16, name=name)
-            nc.sync.dma_start(tile[:], src)
-            return tile
+            list_sb = lists.tile(list(src.shape), U16, name=name)
+            nc.sync.dma_start(list_sb[:], src)
+            return list_sb
 
-        offs_sb = load_list("offs_sb", offs)
-        two_sb = load_list("two_sb", two)
-
-        scale_table = keep.tile([P, T], U8, name="scale_table", align_bytes=64)
-        nc.vector.memset(scale_table[:, 0 : T // 2].bitcast(I32), 0)
-        nc.gpsimd.memset(scale_table[:, T // 2 : T].bitcast(I32), 0)
         def load_weight_half(w, half):
-            raw = keep.tile([P, PACK, H // 2], F32, name="w_raw", tag=f"w_raw{half}", align_bytes=64)
-            cols = slice(half * (H // 2), (half + 1) * (H // 2))
-            nc.sync.dma_start(raw[:], w.rearrange("(p j) c -> p j c", j=PACK)[:, :, cols])
+            raw = keep.tile([P, PACK, C // 2], F32, name="w_raw", tag=f"w_raw{half}", align_bytes=64)
+            nc.sync.dma_start(raw[:], w.rearrange("(p j) c -> p j c", j=PACK)[:, :, HALVES[half]])
             return raw
 
         def interleave(grouped, raw):
@@ -52,26 +55,36 @@ def tile_picked_momorderpagez_none_p_kernel(
                 grouped.rearrange("p (c i) j -> p c j i", i=4), raw.rearrange("p j (c i) -> p c j i", i=4)
             )
 
-        def interleave_weight_half(raw, name):
-            grouped = keep.tile([P, H // 2, PACK], BF16, name=name, tag=name, align_bytes=64)
-            interleave(grouped[:], raw[:])
-            return grouped
-
         def quantize(codes, scales, grouped):
-            nc.vector.quantize_mx(
-                out=codes.bitcast(FP8X4), scales=scales, in_=grouped.rearrange("p c j -> p (c j)")
+            nc.vector.quantize_mx(out=codes.bitcast(FP8X4), scales=scales, in_=grouped.rearrange("p c j -> p (c j)"))
+
+        def product(acc, l_codes, l_scales, r_codes, r_scales):
+            nc.tensor.matmul_mx(
+                out=acc,
+                lhsT=l_codes.bitcast(FP8X4),
+                lhsT_scale=l_scales,
+                rhs=r_codes.bitcast(FP8X4),
+                rhs_scale=r_scales,
+                start=True,
+                stop=True,
             )
 
+        offs_sb = load_list("offs_sb", offs)
+        two_sb = load_list("two_sb", two)
+
+        scale_table = keep.tile([P, T], U8, name="scale_table", align_bytes=64)
+        nc.vector.memset(scale_table[:, 0 : T // 2].bitcast(I32), 0)
+        nc.gpsimd.memset(scale_table[:, T // 2 : T].bitcast(I32), 0)
         wa_raw = [load_weight_half(wa, 0)]
-        for q in range(4):
+        for q in range(P // QUADRANT):
             nc.sync.dma_start(
-                scale_table[32 * q : 32 * q + 4, :].bitcast(I32),
+                scale_table[QUADRANT * q : QUADRANT * q + 4, :].bitcast(I32),
                 x_scales[0][4 * q : 4 * q + 4, :].bitcast(I32),
             )
         wa_raw.append(load_weight_half(wa, 1))
 
-        word_table = keep.tile([P, T], U32, name="word_table", tag="word_table", align_bytes=64)
-        nc.sync.dma_start(word_table[:].bitcast(I32), x_words[0].rearrange("p n t -> p (n t)").bitcast(I32))
+        word_table = keep.tile([P, T], U32, name="word_table", align_bytes=64)
+        nc.sync.dma_start(word_table[:].bitcast(I32), x_words[0].rearrange("p n j -> p (n j)").bitcast(I32))
 
         n1_sb = load_list("n1_sb", n1)
         n2_sb = load_list("n2_sb", n2)
@@ -82,180 +95,173 @@ def tile_picked_momorderpagez_none_p_kernel(
         nc.gpsimd.memset(g_rows[:], 0.0)
         for i, g in enumerate((gt, gi)):
             nc.sync.dma_start(
-                g_rows[PACK * i : PACK * (i + 1), :].rearrange("t (b r) -> t b r", r=8),
-                g.rearrange("(b t r) o -> t b (r o)", t=PACK, r=8),
+                g_rows[PACK * i : PACK * (i + 1), :].rearrange("t (c r) -> t c r", r=RUN),
+                g.rearrange("(c t r) o -> t c (r o)", t=PACK, r=RUN),
             )
         n4_sb = load_list("n4_sb", n4)
         n3_sb = load_list("n3_sb", n3)
 
-        pages = [keep.tile([P, U], F32, name="page0")]
+        pages = [keep.tile([P, PAGE], F32, name="page0")]
         nc.vector.memset(pages[0][:].bitcast(I32), 0)
 
-        def blank_page(tag):
-            page = keep.tile([P, U], F32, name="page", tag=tag, align_bytes=64)
-            nc.sync.dma_start(page[:], pages[0][:])
-            pages.append(page)
+        wa_grouped = []
+        for half in range(2):
+            grouped = keep.tile([P, C // 2, PACK], BF16, name=f"wa_grouped{half}", align_bytes=64)
+            interleave(grouped[:], wa_raw[half][:])
+            wa_grouped.append(grouped)
 
-        wa_grouped = [interleave_weight_half(wa_raw[h], f"wa_grouped{h}") for h in range(2)]
-
-        def pick_scales(name, list_sb, tag):
-            picked = keep.tile([P, S], U8, name="picked", tag=tag, align_bytes=64)
+        def pick_scales(name, list_sb):
+            picked = keep.tile([P, S], U8, name=name, align_bytes=64)
             nc.vector.tensor_copy(picked[:], scale_table[:].indirect(list_sb[:]))
-            dealt = keep.tile([P, S], U8, name=name, align_bytes=64)
-            return picked, dealt
+            return picked
 
         def deal_scales(picked, dealt):
             nc.vector.tensor_copy(
-                dealt[:].bitcast(I32).rearrange("p (t b w) -> p t b w", t=PACK, w=2),
-                picked[:].bitcast(I32).rearrange("p (b t w) -> p t b w", t=PACK, w=2),
+                dealt[:].bitcast(I32).rearrange("p (t c w) -> p t c w", t=PACK, w=2),
+                picked[:].bitcast(I32).rearrange("p (c t w) -> p t c w", t=PACK, w=2),
             )
-
-        xa_picked, xa_scales = pick_scales("xa_scales", offs_sb, "xa_picked")
-        xb_picked, xb_scales = pick_scales("xb_scales", two_sb, "xb_picked")
-
-        wa_codes = keep.tile([P, H], U32, name="wa_codes", tag="wa_codes", align_bytes=64)
-        wa_scales = keep.tile([P, H], U8, name="wa_scales", align_bytes=64)
-        for h in range(2):
-            cols = slice(h * (H // 2), (h + 1) * (H // 2))
-            quantize(wa_codes[:, cols], wa_scales[:, cols], wa_grouped[h][:])
-
-        deal_scales(xa_picked, xa_scales)
-        deal_scales(xb_picked, xb_scales)
 
         def pick_words(name, list_sb, tag):
             picked = keep.tile([P, S], U32, name=name, tag=tag, align_bytes=64)
             nc.vector.tensor_copy(
-                picked[:].rearrange("p (t b r) -> p b t r", t=PACK, r=8),
+                picked[:].rearrange("p (t c r) -> p c t r", t=PACK, r=RUN),
                 word_table[:].indirect(list_sb[:]),
             )
             return picked
 
-        xa_words = pick_words("xa_words", offs_sb, "xa_wb_dt1")
-        xb_words = pick_words("xb_words", two_sb, "xb_words")
+        xa_picked = pick_scales("xa_picked", offs_sb)
+        xa_scales = keep.tile([P, S], U8, name="xa_scales", align_bytes=64)
+        xb_picked = pick_scales("xb_picked", two_sb)
+        xb_scales = keep.tile([P, S], U8, name="xb_scales", align_bytes=64)
 
-        def mx(acc, l_codes, l_scales, r_codes, r_scales):
-            nc.tensor.matmul_mx(
-                out=acc, lhsT=l_codes.bitcast(FP8X4), lhsT_scale=l_scales,
-                rhs=r_codes.bitcast(FP8X4), rhs_scale=r_scales, start=True, stop=True,
-            )
+        wa_codes = keep.tile([P, C], U32, name="wa_codes", tag="wa_codes", align_bytes=64)
+        wa_scales = keep.tile([P, C], U8, name="wa_scales", align_bytes=64)
+        for half in range(2):
+            quantize(wa_codes[:, HALVES[half]], wa_scales[:, HALVES[half]], wa_grouped[half][:])
+
+        deal_scales(xa_picked, xa_scales)
+        deal_scales(xb_picked, xb_scales)
+        xa_words = pick_words("xa_words", offs_sb, "xa_wb_ordered")
+        xb_words = pick_words("xb_words", two_sb, "xb_words")
 
         a_sb = []
         for t in range(PACK):
-            cols = slice(t * P, (t + 1) * P)
-            a_t = keep.tile([P, H], F32, name=f"a{t}", tag=f"a{t}", align_bytes=64)
-            for part in ((slice(0, H // 2), slice(H // 2, H)) if t == 0 else (slice(0, H),)):
-                acc = psum.tile([P, part.stop - part.start], F32, name="acc", tag="acc", bufs=4)
-                mx(acc[:], xa_words[:, cols], xa_scales[:, cols], wa_codes[:, part], wa_scales[:, part])
-                nc.scalar.copy(a_t[:, part], acc[:])
+            places = slice(t * P, (t + 1) * P)
+            a_t = keep.tile([P, C], F32, name=f"a{t}", tag=f"a{t}", align_bytes=64)
+            for cols in HALVES if t == 0 else (slice(0, C),):
+                acc = psum.tile([P, cols.stop - cols.start], F32, name="acc", tag="wide", bufs=WIDE_BANKS)
+                product(acc[:], xa_words[:, places], xa_scales[:, places], wa_codes[:, cols], wa_scales[:, cols])
+                nc.scalar.copy(a_t[:, cols], acc[:])
             a_sb.append(a_t)
 
-        wb_raw = [load_weight_half(wb, h) for h in range(2)]
-        wb_grouped = keep.tile([P, N, PACK], BF16, name="wb_grouped", tag="xa_wb_dt1", align_bytes=64)
-        for h in range(2):
-            interleave(wb_grouped[:, h * (N // 2) : (h + 1) * (N // 2), :], wb_raw[h][:])
+        wb_raw = [load_weight_half(wb, half) for half in range(2)]
+        wb_grouped = keep.tile([P, C, PACK], BF16, name="wb_grouped", tag="xa_wb_ordered", align_bytes=64)
+        for half in range(2):
+            interleave(wb_grouped[:, HALVES[half], :], wb_raw[half][:])
+
         g_psum = psum.tile([P, P], F32, name="g_psum")
         nc.tensor.transpose(g_psum[:], g_rows[:], ident[:])
         g_cols = keep.tile([P, 2 * PACK], F32, name="g_cols", tag="w_raw1", align_bytes=64)
         nc.scalar.copy(g_cols[:], g_psum[:, 0 : 2 * PACK])
-        wb_codes = keep.tile([P, N], U32, name="wb_codes", align_bytes=64)
-        wb_scales = keep.tile([P, N], U8, name="wb_scales", align_bytes=64)
-        z2_grouped = keep.tile([P, N, PACK], BF16, name="z2_grouped", align_bytes=64)
-        z2_codes = keep.tile([P, N], U32, name="z2_codes", align_bytes=64)
-        z2_scales = keep.tile([P, N], U8, name="z2_scales", align_bytes=64)
+
+        wb_codes = keep.tile([P, C], U32, name="wb_codes", align_bytes=64)
+        wb_scales = keep.tile([P, C], U8, name="wb_scales", align_bytes=64)
+        z2_grouped = keep.tile([P, C, PACK], BF16, name="z2_grouped", align_bytes=64)
+        z2_codes = keep.tile([P, C], U32, name="z2_codes", align_bytes=64)
+        z2_scales = keep.tile([P, C], U8, name="z2_scales", align_bytes=64)
 
         def second_projection():
             quantize(wb_codes[:], wb_scales[:], wb_grouped[:])
             for t in range(PACK):
-                acc_b = psum.tile([P, N], F32, name="acc_b", tag="acc_b", bufs=3)
-                mx(acc_b[:], xb_words[:, t * P : (t + 1) * P], xb_scales[:, t * P : (t + 1) * P],
-                   wb_codes[:], wb_scales[:])
+                places = slice(t * P, (t + 1) * P)
+                acc_b = psum.tile([P, C], F32, name="acc_b", tag="side", bufs=SIDE_BANKS)
+                product(acc_b[:], xb_words[:, places], xb_scales[:, places], wb_codes[:], wb_scales[:])
                 nc.scalar.activation(z2_grouped[:, :, t], acc_b[:], ACT.Copy, scale=g_cols[:, PACK + t : PACK + t + 1])
 
-        pa = keep.tile([P, W], F32, name="pa")
-        pb = keep.tile([P, W], F32, name="pb")
-        ra = keep.tile([P, W], F32, name="ra")
-        rb = keep.tile([P, W], F32, name="rb")
-        dt = []
-        z_grouped = [keep.tile([P, P, PACK], BF16, name=f"z_grouped{u}", tag=f"z_grouped{u}", align_bytes=64) for u in range(PACK)]
+        def blank_page(tag):
+            page = keep.tile([P, PAGE], F32, name="page", tag=tag, align_bytes=64)
+            nc.sync.dma_start(page[:], pages[0][:])
+            pages.append(page)
 
-        def fetch_pairs(t):
-            nc.vector.tensor_copy(pa[:], a_sb[t][:].indirect(n1_sb[:]))
+        pa = [keep.tile([P, PAIRS], F32, name=f"pa{i}") for i in range(2)]
+        pb = keep.tile([P, PAIRS], F32, name="pb")
+        ordered = keep.tile([P, 2 * PAIRS], F32, name="first_ordered")
+        dt = [keep.tile([P, C], F32, name=f"dt{t}") for t in range(PACK)]
+        z_grouped = [keep.tile([P, P, PACK], BF16, name=f"z_grouped{u}", align_bytes=64) for u in range(PACK)]
+        larger, smaller = slice(0, PAIRS), slice(PAIRS, 2 * PAIRS)
+
+        def fetch_pa(t):
+            nc.vector.tensor_copy(pa[t % 2][:], a_sb[t][:].indirect(n1_sb[:]))
+
+        def fetch_pb(t):
             nc.vector.tensor_copy(pb[:], a_sb[t][:].indirect(n2_sb[:]))
 
-        def order_pairs(t):
-            nc.vector.tensor_tensor(ra[:], pa[:], pb[:], ALU.max)
-            nc.vector.tensor_tensor(rb[:], pa[:], pb[:], ALU.min)
-
         def round_z(t):
-            by_tile = dt[t][:].rearrange("p (m u) -> p u m", u=PACK)
+            by_row_tile = dt[t][:].rearrange("p (m u) -> p u m", u=PACK)
             for u in range(PACK):
-                nc.scalar.activation(z_grouped[u][:, :, t], by_tile[:, u, :], ACT.Copy, scale=g_cols[:, t : t + 1])
+                nc.scalar.activation(z_grouped[u][:, :, t], by_row_tile[:, u, :], ACT.Copy, scale=g_cols[:, t : t + 1])
 
-        fetch_pairs(0)
-        order_pairs(0)
+        fetch_pa(0)
+        fetch_pb(0)
         for t in range(PACK):
-            dt.append(keep.tile([P, H], F32, name=f"dt{t}", tag="xa_wb_dt1" if t == 1 else f"dt{t}", align_bytes=64))
-            nc.vector.tensor_copy(dt[t][:].indirect(n1_sb[:]), ra[:])
             if t + 1 < PACK:
-                fetch_pairs(t + 1)
-            nc.vector.tensor_copy(dt[t][:].indirect(n2_sb[:]), rb[:])
+                fetch_pa(t + 1)
+            nc.vector.tensor_tensor(ordered[:, larger], pa[t % 2][:], pb[:], ALU.max)
+            nc.vector.tensor_tensor(ordered[:, smaller], pa[t % 2][:], pb[:], ALU.min)
+            nc.vector.tensor_copy(dt[t][:].indirect(n1_sb[:]), ordered[:, larger])
             if t + 1 < PACK:
-                order_pairs(t + 1)
+                fetch_pb(t + 1)
+            nc.vector.tensor_copy(dt[t][:].indirect(n2_sb[:]), ordered[:, smaller])
             if t == 0:
                 second_projection()
                 for tag in ("w_raw0", "wa_codes", "a0"):
                     blank_page(tag)
+                ordered = keep.tile([P, 2 * PAIRS], F32, name="ordered", tag="xa_wb_ordered", align_bytes=64)
             round_z(t)
 
         quantize(z2_codes[:], z2_scales[:], z2_grouped[:])
 
         z_codes = [keep.tile([P, P], U32, name=f"z_codes{u}", align_bytes=64) for u in range(PACK)]
         z_scales = [keep.tile([P, P], U8, name=f"z_scales{u}", align_bytes=64) for u in range(PACK)]
-        neg_relu = [keep.tile([P, N], F32, name=f"neg_relu{u}") for u in range(PACK)]
-        fetched = [keep.tile([P, N], F32, name=f"fetched{u}") for u in range(PACK)]
-        half = N // 2
-        halves = [slice(h * half, (h + 1) * half) for h in range(2)]
+        neg_relu = [keep.tile([P, C], F32, name=f"neg_relu{u}") for u in range(PACK)]
+        fetched = [keep.tile([P, C], F32, name=f"fetched{u}") for u in range(PACK)]
         sums = []
         cv = []
 
         def copy_cv(u):
-            cv_u = keep.tile([P, N], F32, name="cv", tag=f"relu{u + 1}")
-            for cols, acc in sums[u]:
-                nc.scalar.activation(cv_u[:, cols], acc[:], ACT.Copy, scale=CV_SCALE)
+            cv_u = keep.tile([P, C], F32, name="cv", tag=f"relu{u + 1}")
+            for cols, acc_cv in sums[u]:
+                nc.scalar.activation(cv_u[:, cols], acc_cv[:], ACT.Copy, scale=CV_SCALE)
             cv.append(cv_u)
 
         for u in range(PACK):
             quantize(z_codes[u][:], z_scales[u][:], z_grouped[u][:])
             if u == 0:
                 sums.append([])
-                for cols in halves:
-                    acc = psum.tile([P, half], F32, name="acc_b", tag="acc_b", bufs=3)
-                    mx(acc[:], z_codes[u][:], z_scales[u][:], z2_codes[:, cols], z2_scales[:, cols])
-                    nc.vector.tensor_scalar(neg_relu[u][:, cols], acc[:], -CV_SCALE, 0.0, ALU.mult, ALU.min)
-                    sums[u].append((cols, acc))
+                for cols in HALVES:
+                    acc_cv = psum.tile([P, C // 2], F32, name="acc_cv", tag="side", bufs=SIDE_BANKS)
+                    product(acc_cv[:], z_codes[u][:], z_scales[u][:], z2_codes[:, cols], z2_scales[:, cols])
+                    nc.vector.tensor_scalar(neg_relu[u][:, cols], acc_cv[:], -CV_SCALE, 0.0, ALU.mult, ALU.min)
+                    sums[u].append((cols, acc_cv))
             else:
-                acc = psum.tile([P, N], F32, name="acc", tag="acc", bufs=4)
-                mx(acc[:], z_codes[u][:], z_scales[u][:], z2_codes[:], z2_scales[:])
-                sums.append([(slice(0, N), acc)])
-                relu = keep.tile([P, N], F32, name="relu", tag=f"relu{u}")
-                nc.scalar.activation(relu[:], acc[:], ACT.Relu, scale=CV_SCALE)
+                acc_cv = psum.tile([P, C], F32, name="acc_cv", tag="wide", bufs=WIDE_BANKS)
+                product(acc_cv[:], z_codes[u][:], z_scales[u][:], z2_codes[:], z2_scales[:])
+                sums.append([(slice(0, C), acc_cv)])
+                relu = keep.tile([P, C], F32, name="relu", tag=f"relu{u}")
+                nc.scalar.activation(relu[:], acc_cv[:], ACT.Relu, scale=CV_SCALE)
                 nc.scalar.activation(neg_relu[u][:], relu[:], ACT.Copy, scale=-1.0)
                 copy_cv(u - 1)
         copy_cv(PACK - 1)
 
-        list_cols = half // 16
-
-        def fetch(u):
-            for h in range(2):
-                nc.vector.tensor_copy(
-                    fetched[u][:, halves[h]],
-                    neg_relu[u][:].indirect(n4_sb[:, h * list_cols : (h + 1) * list_cols]),
-                )
+        def fetch_neg_relu(u):
+            for cols in HALVES:
+                entries = n4_sb[:, cols.start // LIST_ROWS : cols.stop // LIST_ROWS]
+                nc.vector.tensor_copy(fetched[u][:, cols], neg_relu[u][:].indirect(entries))
 
         out_rows = out.rearrange("(m u) w -> u m w", u=PACK)
-        fetch(0)
+        fetch_neg_relu(0)
         for u in range(PACK):
             if u + 1 < PACK:
-                fetch(u + 1)
+                fetch_neg_relu(u + 1)
             nc.vector.tensor_tensor(pages[u][:].indirect(n3_sb[:]), fetched[u][:], cv[u][:], ALU.add)
             nc.sync.dma_start(out_rows[u], pages[u][:])

@@ -256,12 +256,18 @@ def tile_picked_momorderpagez_none_p_kernel(
         def fetch_neg_relu(u):
             for cols in HALVES:
                 entries = n4_sb[:, cols.start // LIST_ROWS : cols.stop // LIST_ROWS]
-                nc.vector.tensor_copy(fetched[u][:, cols], neg_relu[u][:].indirect(entries))
+                if u < 2:
+                    nc.vector.tensor_copy(fetched[u][:, cols], neg_relu[u][:].indirect(entries))
+                else:
+                    nc.vector.tensor_tensor(fetched[u][:, cols], neg_relu[u][:].indirect(entries), cv[u][:, cols], ALU.add)
 
         out_rows = out.rearrange("(m u) w -> u m w", u=PACK)
         fetch_neg_relu(0)
         for u in range(PACK):
             if u + 1 < PACK:
                 fetch_neg_relu(u + 1)
-            nc.vector.tensor_tensor(pages[u][:].indirect(n3_sb[:]), fetched[u][:], cv[u][:], ALU.add)
+            if u < 2:
+                nc.vector.tensor_tensor(pages[u][:].indirect(n3_sb[:]), fetched[u][:], cv[u][:], ALU.add)
+            else:
+                nc.vector.tensor_copy(pages[u][:].indirect(n3_sb[:]), fetched[u][:])
             nc.sync.dma_start(out_rows[u], pages[u][:])

from contextlib import ExitStack

import concourse.mybir as mybir
from concourse.masks import make_identity

F32 = mybir.dt.float32
BF16 = mybir.dt.bfloat16
I32 = mybir.dt.int32
U32 = mybir.dt.uint32
U16 = mybir.dt.uint16
U8 = mybir.dt.uint8
FP8X4 = mybir.dt.float8_e4m3fn_x4
ALU = mybir.AluOpType
ACT = mybir.ActivationFunctionType

P = 128
PACK = 4
RUN = 8
QUADRANT = 32
LIST_ROWS = 16
T = 2048
S = 512
C = 512
PAIRS = 256
PAGE = 1024
CV_SCALE = 0.0625
HALVES = (slice(0, C // 2), slice(C // 2, C))
WIDE_BANKS = 4
SIDE_BANKS = 3

FLOPS = 3 * 2 * 512 * 512 * 512


def tile_picked_momorderpagez_none_p_kernel(
    tc, x_words, x_scales, wa, wb, gt, gi, offs, two, n1, n2, n3, n4, out
):
    nc = tc.nc
    with ExitStack() as ctx:
        lists = ctx.enter_context(tc.tile_pool(name="lists", bufs=1))
        keep = ctx.enter_context(tc.tile_pool(name="keep", bufs=1))
        psum = ctx.enter_context(tc.psum_pool(name="psum", bufs=1))

        def load_list(name, src):
            list_sb = lists.tile(list(src.shape), U16, name=name)
            nc.sync.dma_start(list_sb[:], src)
            return list_sb

        def load_weight_half(w, half):
            raw = keep.tile([P, PACK, C // 2], F32, name="w_raw", tag=f"w_raw{half}", align_bytes=64)
            nc.sync.dma_start(raw[:], w.rearrange("(p j) c -> p j c", j=PACK)[:, :, HALVES[half]])
            return raw

        def interleave(grouped, raw):
            nc.scalar.copy(
                grouped.rearrange("p (c i) j -> p c j i", i=4), raw.rearrange("p j (c i) -> p c j i", i=4)
            )

        def quantize(codes, scales, grouped):
            nc.vector.quantize_mx(out=codes.bitcast(FP8X4), scales=scales, in_=grouped.rearrange("p c j -> p (c j)"))

        def product(acc, l_codes, l_scales, r_codes, r_scales):
            nc.tensor.matmul_mx(
                out=acc,
                lhsT=l_codes.bitcast(FP8X4),
                lhsT_scale=l_scales,
                rhs=r_codes.bitcast(FP8X4),
                rhs_scale=r_scales,
                start=True,
                stop=True,
            )

        offs_sb = load_list("offs_sb", offs)
        two_sb = load_list("two_sb", two)

        scale_table = keep.tile([P, T], U8, name="scale_table", align_bytes=64)
        nc.vector.memset(scale_table[:, 0 : T // 2].bitcast(I32), 0)
        nc.gpsimd.memset(scale_table[:, T // 2 : T].bitcast(I32), 0)
        wa_raw = [load_weight_half(wa, 0)]
        for q in range(P // QUADRANT):
            nc.sync.dma_start(
                scale_table[QUADRANT * q : QUADRANT * q + 4, :].bitcast(I32),
                x_scales[0][4 * q : 4 * q + 4, :].bitcast(I32),
            )
        wa_raw.append(load_weight_half(wa, 1))

        word_table = keep.tile([P, T], U32, name="word_table", align_bytes=64)
        nc.sync.dma_start(word_table[:].bitcast(I32), x_words[0].rearrange("p n j -> p (n j)").bitcast(I32))

        n1_sb = load_list("n1_sb", n1)
        n2_sb = load_list("n2_sb", n2)

        ident = keep.tile([P, P], F32, name="ident")
        make_identity(nc, ident[:])
        g_rows = keep.tile([P, P], F32, name="g_rows")
        nc.gpsimd.memset(g_rows[:], 0.0)
        for i, g in enumerate((gt, gi)):
            nc.sync.dma_start(
                g_rows[PACK * i : PACK * (i + 1), :].rearrange("t (c r) -> t c r", r=RUN),
                g.rearrange("(c t r) o -> t c (r o)", t=PACK, r=RUN),
            )
        n4_sb = load_list("n4_sb", n4)
        n3_sb = load_list("n3_sb", n3)

        pages = [keep.tile([P, PAGE], F32, name="page0")]
        nc.vector.memset(pages[0][:].bitcast(I32), 0)

        wa_grouped = []
        for half in range(2):
            grouped = keep.tile([P, C // 2, PACK], BF16, name=f"wa_grouped{half}", align_bytes=64)
            interleave(grouped[:], wa_raw[half][:])
            wa_grouped.append(grouped)

        def pick_scales(name, list_sb):
            picked = keep.tile([P, S], U8, name=name, align_bytes=64)
            nc.vector.tensor_copy(picked[:], scale_table[:].indirect(list_sb[:]))
            return picked

        def deal_scales(picked, dealt):
            nc.vector.tensor_copy(
                dealt[:].bitcast(I32).rearrange("p (t c w) -> p t c w", t=PACK, w=2),
                picked[:].bitcast(I32).rearrange("p (c t w) -> p t c w", t=PACK, w=2),
            )

        def pick_words(name, list_sb, tag):
            picked = keep.tile([P, S], U32, name=name, tag=tag, align_bytes=64)
            nc.vector.tensor_copy(
                picked[:].rearrange("p (t c r) -> p c t r", t=PACK, r=RUN),
                word_table[:].indirect(list_sb[:]),
            )
            return picked

        xa_picked = pick_scales("xa_picked", offs_sb)
        xa_scales = keep.tile([P, S], U8, name="xa_scales", align_bytes=64)
        xb_picked = pick_scales("xb_picked", two_sb)
        xb_scales = keep.tile([P, S], U8, name="xb_scales", align_bytes=64)

        wa_codes = keep.tile([P, C], U32, name="wa_codes", tag="wa_codes", align_bytes=64)
        wa_scales = keep.tile([P, C], U8, name="wa_scales", align_bytes=64)
        for half in range(2):
            quantize(wa_codes[:, HALVES[half]], wa_scales[:, HALVES[half]], wa_grouped[half][:])

        deal_scales(xa_picked, xa_scales)
        deal_scales(xb_picked, xb_scales)
        xa_words = pick_words("xa_words", offs_sb, "xa_wb_ordered")
        xb_words = pick_words("xb_words", two_sb, "xb_words")

        a_sb = []
        for t in range(PACK):
            places = slice(t * P, (t + 1) * P)
            a_t = keep.tile([P, C], F32, name=f"a{t}", tag=f"a{t}", align_bytes=64)
            for cols in HALVES if t == 0 else (slice(0, C),):
                acc = psum.tile([P, cols.stop - cols.start], F32, name="acc", tag="wide", bufs=WIDE_BANKS)
                product(acc[:], xa_words[:, places], xa_scales[:, places], wa_codes[:, cols], wa_scales[:, cols])
                nc.scalar.copy(a_t[:, cols], acc[:])
            a_sb.append(a_t)

        wb_raw = [load_weight_half(wb, half) for half in range(2)]
        wb_grouped = keep.tile([P, C, PACK], BF16, name="wb_grouped", tag="xa_wb_ordered", align_bytes=64)
        for half in range(2):
            interleave(wb_grouped[:, HALVES[half], :], wb_raw[half][:])

        g_psum = psum.tile([P, P], F32, name="g_psum")
        nc.tensor.transpose(g_psum[:], g_rows[:], ident[:])
        g_cols = keep.tile([P, 2 * PACK], F32, name="g_cols", tag="w_raw1", align_bytes=64)
        nc.scalar.copy(g_cols[:], g_psum[:, 0 : 2 * PACK])

        wb_codes = keep.tile([P, C], U32, name="wb_codes", align_bytes=64)
        wb_scales = keep.tile([P, C], U8, name="wb_scales", align_bytes=64)
        z2_grouped = keep.tile([P, C, PACK], BF16, name="z2_grouped", align_bytes=64)
        z2_codes = keep.tile([P, C], U32, name="z2_codes", align_bytes=64)
        z2_scales = keep.tile([P, C], U8, name="z2_scales", align_bytes=64)

        def second_projection():
            quantize(wb_codes[:], wb_scales[:], wb_grouped[:])
            for t in range(PACK):
                places = slice(t * P, (t + 1) * P)
                acc_b = psum.tile([P, C], F32, name="acc_b", tag="side", bufs=SIDE_BANKS)
                product(acc_b[:], xb_words[:, places], xb_scales[:, places], wb_codes[:], wb_scales[:])
                nc.scalar.activation(z2_grouped[:, :, t], acc_b[:], ACT.Copy, scale=g_cols[:, PACK + t : PACK + t + 1])

        def blank_page(tag):
            page = keep.tile([P, PAGE], F32, name="page", tag=tag, align_bytes=64)
            nc.sync.dma_start(page[:], pages[0][:])
            pages.append(page)

        pa = [keep.tile([P, PAIRS], F32, name=f"pa{i}") for i in range(2)]
        pb = keep.tile([P, PAIRS], F32, name="pb")
        ordered = keep.tile([P, 2 * PAIRS], F32, name="first_ordered")
        dt = [keep.tile([P, C], F32, name=f"dt{t}") for t in range(PACK)]
        z_grouped = [keep.tile([P, P, PACK], BF16, name=f"z_grouped{u}", align_bytes=64) for u in range(PACK)]
        larger, smaller = slice(0, PAIRS), slice(PAIRS, 2 * PAIRS)

        def fetch_pa(t):
            nc.vector.tensor_copy(pa[t % 2][:], a_sb[t][:].indirect(n1_sb[:]))

        def fetch_pb(t):
            nc.vector.tensor_copy(pb[:], a_sb[t][:].indirect(n2_sb[:]))

        def round_z(t):
            by_row_tile = dt[t][:].rearrange("p (m u) -> p u m", u=PACK)
            for u in range(PACK):
                nc.scalar.activation(z_grouped[u][:, :, t], by_row_tile[:, u, :], ACT.Copy, scale=g_cols[:, t : t + 1])

        fetch_pa(0)
        fetch_pb(0)
        for t in range(PACK):
            if t + 1 < PACK:
                fetch_pa(t + 1)
            nc.vector.tensor_tensor(ordered[:, larger], pa[t % 2][:], pb[:], ALU.max)
            nc.vector.tensor_tensor(ordered[:, smaller], pa[t % 2][:], pb[:], ALU.min)
            nc.vector.tensor_copy(dt[t][:].indirect(n1_sb[:]), ordered[:, larger])
            if t + 1 < PACK:
                fetch_pb(t + 1)
            nc.vector.tensor_copy(dt[t][:].indirect(n2_sb[:]), ordered[:, smaller])
            if t == 0:
                second_projection()
                for tag in ("w_raw0", "wa_codes", "a0"):
                    blank_page(tag)
                ordered = keep.tile([P, 2 * PAIRS], F32, name="ordered", tag="xa_wb_ordered", align_bytes=64)
            round_z(t)

        quantize(z2_codes[:], z2_scales[:], z2_grouped[:])

        z_codes = [keep.tile([P, P], U32, name=f"z_codes{u}", align_bytes=64) for u in range(PACK)]
        z_scales = [keep.tile([P, P], U8, name=f"z_scales{u}", align_bytes=64) for u in range(PACK)]
        neg_relu = [keep.tile([P, C], F32, name=f"neg_relu{u}") for u in range(PACK)]
        fetched = [keep.tile([P, C], F32, name=f"fetched{u}") for u in range(PACK)]
        sums = []
        cv = []

        def copy_cv(u):
            cv_u = keep.tile([P, C], F32, name="cv", tag=f"relu{u + 1}")
            for cols, acc_cv in sums[u]:
                nc.scalar.activation(cv_u[:, cols], acc_cv[:], ACT.Copy, scale=CV_SCALE)
            cv.append(cv_u)

        for u in range(PACK):
            quantize(z_codes[u][:], z_scales[u][:], z_grouped[u][:])
            if u == 0:
                sums.append([])
                for cols in HALVES:
                    acc_cv = psum.tile([P, C // 2], F32, name="acc_cv", tag="side", bufs=SIDE_BANKS)
                    product(acc_cv[:], z_codes[u][:], z_scales[u][:], z2_codes[:, cols], z2_scales[:, cols])
                    nc.vector.tensor_scalar(neg_relu[u][:, cols], acc_cv[:], -CV_SCALE, 0.0, ALU.mult, ALU.min)
                    sums[u].append((cols, acc_cv))
            else:
                acc_cv = psum.tile([P, C], F32, name="acc_cv", tag="wide", bufs=WIDE_BANKS)
                product(acc_cv[:], z_codes[u][:], z_scales[u][:], z2_codes[:], z2_scales[:])
                sums.append([(slice(0, C), acc_cv)])
                relu = keep.tile([P, C], F32, name="relu", tag=f"relu{u}")
                nc.scalar.activation(relu[:], acc_cv[:], ACT.Relu, scale=CV_SCALE)
                nc.scalar.activation(neg_relu[u][:], relu[:], ACT.Copy, scale=-1.0)
                copy_cv(u - 1)
        copy_cv(PACK - 1)

        def fetch_neg_relu(u):
            for cols in HALVES:
                entries = n4_sb[:, cols.start // LIST_ROWS : cols.stop // LIST_ROWS]
                if u < 2:
                    nc.vector.tensor_copy(fetched[u][:, cols], neg_relu[u][:].indirect(entries))
                else:
                    nc.vector.tensor_tensor(fetched[u][:, cols], neg_relu[u][:].indirect(entries), cv[u][:, cols], ALU.add)

        out_rows = out.rearrange("(m u) w -> u m w", u=PACK)
        fetch_neg_relu(0)
        for u in range(PACK):
            if u + 1 < PACK:
                fetch_neg_relu(u + 1)
            if u < 2:
                nc.vector.tensor_tensor(pages[u][:].indirect(n3_sb[:]), fetched[u][:], cv[u][:], ALU.add)
            else:
                nc.vector.tensor_copy(pages[u][:].indirect(n3_sb[:]), fetched[u][:])
            nc.sync.dma_start(out_rows[u], pages[u][:])
